import numpy as np
import ml_dtypes


def mxq(x, axis, fmt="e4m3"):
    dtype, down = {"e4m3": (ml_dtypes.float8_e4m3fn, 7), "e5m2": (ml_dtypes.float8_e5m2, 14)}[fmt]
    v = np.moveaxis(np.asarray(x, np.float32).astype(ml_dtypes.bfloat16).astype(np.float64), axis, -1)
    blocks = v.reshape(v.shape[:-1] + (-1, 32))
    amax = np.abs(blocks).max(-1, keepdims=True)
    byte = np.maximum(np.where(amax > 0, np.frexp(amax)[1] - 1 + 127, 0) - down, 1)
    scale = np.exp2(byte - 127.0)
    codes = (blocks / scale).astype(np.float32).astype(dtype).astype(np.float64)
    return np.moveaxis((codes * scale).reshape(v.shape), -1, axis)


WIDE = False


def mx_kscale(k):
    if not WIDE:
        return np.ones(k)
    levels = np.array([10, -10, 5, -5, 0])
    if k % 512:
        return np.exp2(np.random.permutation(np.resize(levels, k // 32))).repeat(32)
    a = np.empty((k // 512, 16))
    for p in range(k // 512):
        a[p, :8] = np.random.permutation(np.resize(levels, 8))
        for g in range(8):
            far = levels[np.abs(levels - a[p, g]) >= 10]
            a[p, g + 8] = far[np.random.randint(len(far))]
    return np.exp2(a.ravel()).repeat(32)


def f64(x):
    return np.asarray(x).astype(np.float64)


E2M1 = np.array([0.0, 0.5, 1.0, 1.5, 2.0, 3.0, 4.0, 6.0, -0.0, -0.5, -1.0, -1.5, -2.0, -3.0, -4.0, -6.0])


def pack_weight(w, fmt):
    k, n = w.shape
    w = f64(np.asarray(w, np.float32).astype(ml_dtypes.bfloat16)).reshape(k // 32, 32, n)
    amax = np.abs(w).max(1)
    if fmt == "e4m3":
        byte = np.frexp(amax)[1] - 1 + 127 - 7
    else:
        mant, ex = np.frexp(amax / 6.0)
        byte = np.where(mant > 0.5, ex, ex - 1) + 127
    byte = np.clip(np.where(amax > 0, byte, 1), 1, 254)
    scaled = (w * np.exp2(127.0 - byte)[:, None, :]).reshape(k, n).astype(np.float32)
    by_word = np.ascontiguousarray(scaled.reshape(k // 512, 128, 4, n).transpose(0, 1, 3, 2))
    if fmt == "e4m3":
        words = by_word.astype(ml_dtypes.float8_e4m3fn).view(np.uint8)
    else:
        c = by_word.astype(ml_dtypes.float4_e2m1fn).view(np.uint8) & 0xF
        words = (c[..., 0::2] | (c[..., 1::2] << 4)).reshape(k // 512, 128, 2 * n)
    return np.ascontiguousarray(words), np.ascontiguousarray(byte.astype(np.uint8).reshape(k // 512, 16, n))


def unpack_weight(words, scales, fmt):
    g, _, n = scales.shape
    words = np.ascontiguousarray(words).reshape(g, 128, n, -1)
    if fmt == "e4m3":
        vals = words.view(ml_dtypes.float8_e4m3fn).astype(np.float64)
    else:
        nib = np.empty((g, 128, n, 4), np.uint8)
        nib[..., 0::2] = words & 0xF
        nib[..., 1::2] = words >> 4
        vals = E2M1[nib]
    vals = vals * np.repeat(np.exp2(scales.astype(np.float64) - 127.0), 8, axis=1)[..., None]
    return vals.transpose(0, 1, 3, 2).reshape(g * 512, n)


K, L, M, T = 512, 512, 1536, 1024


def setup_inputs():
    n = np.random.standard_normal
    s1 = mx_kscale(K)[:, None]
    s2 = mx_kscale(L)[:, None]
    p_wx = pack_weight(n((K, M)) / np.sqrt(K) / s1, "e2m1")
    p_wc = pack_weight(n((L, M)) / np.sqrt(L) / s2, "e4m3")
    return {
        "x": (n((K, T)) * s1).astype(np.float32),
        "c": (n((L, T)) * s2).astype(np.float32),
        "wx_words": p_wx[0],
        "wx_scales": p_wx[1],
        "wc_words": p_wc[0],
        "wc_scales": p_wc[1],
        "r": (n((1536, 1024))).astype(np.float32),
    }


def reference(x, c, wx_words, wx_scales, wc_words, wc_scales, r):
    x_ = mxq(f64(x), 0, "e4m3")
    c_ = mxq(f64(c), 0, "e4m3")
    wx_ = unpack_weight(wx_words, wx_scales, "e2m1")
    wc_ = unpack_weight(wc_words, wc_scales, "e4m3")
    y = wx_.T @ x_ + wc_.T @ c_
    return f64(r) + y

@@ -1,0 +1,136 @@
+from contextlib import ExitStack
+
+import concourse.mybir as mybir
+
+K, L, M, T = 512, 512, 1536, 1024
+FLOPS = 2 * M * T * (K + L)
+
+F32 = mybir.dt.float32
+BF16 = mybir.dt.bfloat16
+I32 = mybir.dt.int32
+U32 = mybir.dt.uint32
+U8 = mybir.dt.uint8
+FP8X4 = mybir.dt.float8_e4m3fn_x4
+FP4X4 = mybir.dt.float4_e2m1fn_x4
+
+P = 128
+PACK = 4
+ROWS = M // P
+N_TILE = 512
+HALVES = T // N_TILE
+GROUP = 3
+
+
+def tile_mix_skip_fm_res_kernel(
+    tc, x, c, wx_words, wx_scales, wc_words, wc_scales, r, out
+):
+    nc = tc.nc
+    with ExitStack() as ctx:
+        ctx.enter_context(tc.manual_schedule())
+        keep = ctx.enter_context(tc.tile_pool(name="keep", bufs=1))
+        psum = ctx.enter_context(tc.psum_pool(name="psum", bufs=8))
+
+        planes = keep.tile([P, 2, M], U8, name="planes", align_bytes=64)
+        nc.vector.memset(planes[:].rearrange("p a n -> p (a n)").bitcast(I32), 0)
+        for a, scales in enumerate((wx_scales, wc_scales)):
+            for q in range(4):
+                nc.gpsimd.dma_start(
+                    out=planes[32 * q : 32 * q + 4, a, :].bitcast(I32),
+                    in_=scales[0, 4 * q : 4 * q + 4, :].bitcast(I32),
+                )
+
+        wc_raw = keep.tile([P, M], I32, name="wc_raw", align_bytes=64)
+        nc.sync.dma_start(
+            out=wc_raw[:], in_=wc_words.rearrange("a p n i -> (a p) (n i)").bitcast(I32)
+        )
+        wx_raw = keep.tile([P, 2 * M], U8, name="wx_raw", align_bytes=64)
+        nc.sync.dma_start(
+            out=wx_raw[:].bitcast(I32), in_=wx_words.rearrange("a p b -> (a p) b").bitcast(I32)
+        )
+        x_raw = keep.tile([P, PACK, T], F32, name="x_raw", align_bytes=64)
+        nc.sync.dma_start(out=x_raw[:], in_=x.rearrange("(p j) t -> p j t", j=PACK))
+        c_raw = keep.tile([P, PACK, T], F32, name="c_raw", align_bytes=64)
+        nc.sync.dma_start(out=c_raw[:], in_=c.rearrange("(p j) t -> p j t", j=PACK))
+
+        r_rows = r.rearrange("(p s) t -> p s t", s=ROWS)
+        out_rows = out.rearrange("(p s) t -> p s t", s=ROWS)
+        res = []
+        for g in range(ROWS // GROUP):
+            tile = keep.tile([P, GROUP, T], F32, name="res%d" % g, align_bytes=64)
+            nc.sync.dma_start(out=tile[:], in_=r_rows[:, GROUP * g : GROUP * (g + 1), :])
+            res.append(tile)
+
+        wc = keep.tile([P, ROWS, P], I32, name="wc", align_bytes=64)
+        nc.vector.tensor_copy(out=wc[:], in_=wc_raw[:].rearrange("p (m s) -> p s m", s=ROWS))
+        wx = keep.tile([P, ROWS, P, 2], U8, name="wx", align_bytes=64)
+        nc.vector.tensor_copy(
+            out=wx[:], in_=wx_raw[:].rearrange("p (m s b) -> p s m b", s=ROWS, b=2)
+        )
+        w_scales = keep.tile([P, 2, ROWS, P], U8, name="w_scales", align_bytes=64)
+        nc.vector.tensor_copy(
+            out=w_scales[:], in_=planes[:].rearrange("p a (m s) -> p a s m", s=ROWS)
+        )
+
+        grouped = {}
+        codes = {}
+        bytes_ = {}
+        for name in ("x", "c"):
+            for h in range(HALVES):
+                key = (name, h)
+                grouped[key] = keep.tile(
+                    [P, N_TILE, PACK], BF16, name="grouped_%s%d" % key, align_bytes=64
+                )
+                codes[key] = keep.tile([P, N_TILE], U32, name="codes_%s%d" % key, align_bytes=64)
+                bytes_[key] = keep.tile([P, N_TILE], U8, name="bytes_%s%d" % key, align_bytes=64)
+
+        def interleave(copy, raw, key):
+            h = key[1]
+            copy(
+                out=grouped[key][:],
+                in_=raw[:, :, h * N_TILE : (h + 1) * N_TILE].rearrange("p j t -> p t j"),
+            )
+
+        def quantize(key):
+            nc.vector.quantize_mx(
+                out=codes[key][:].bitcast(FP8X4),
+                scales=bytes_[key][:],
+                in_=grouped[key][:].rearrange("p t j -> p (t j)"),
+            )
+
+        interleave(nc.scalar.copy, x_raw, ("x", 0))
+        interleave(nc.scalar.copy, x_raw, ("x", 1))
+        interleave(nc.scalar.copy, c_raw, ("c", 1))
+        quantize(("x", 0))
+        interleave(nc.vector.tensor_copy, c_raw, ("c", 0))
+        quantize(("x", 1))
+        quantize(("c", 0))
+        quantize(("c", 1))
+
+        for s in range(ROWS):
+            g, i = divmod(s, GROUP)
+            for h in range(HALVES):
+                acc = psum.tile([P, N_TILE], F32, name="acc")
+                nc.tensor.matmul_mx(
+                    out=acc[:],
+                    lhsT=wx[:, s, :, :].rearrange("p m b -> p (m b)").bitcast(FP4X4),
+                    lhsT_scale=w_scales[:, 0, s, :],
+                    rhs=codes["x", h][:].bitcast(FP8X4),
+                    rhs_scale=bytes_["x", h][:],
+                    start=True,
+                    stop=False,
+                )
+                nc.tensor.matmul_mx(
+                    out=acc[:],
+                    lhsT=wc[:, s, :].bitcast(FP8X4),
+                    lhsT_scale=w_scales[:, 1, s, :],
+                    rhs=codes["c", h][:].bitcast(FP8X4),
+                    rhs_scale=bytes_["c", h][:],
+                    start=False,
+                    stop=True,
+                )
+                part = res[g][:, i, h * N_TILE : (h + 1) * N_TILE]
+                nc.vector.tensor_tensor(out=part, in0=acc[:], in1=part, op=mybir.AluOpType.add)
+            if i == GROUP - 1:
+                nc.sync.dma_start(
+                    out=out_rows[:, GROUP * g : GROUP * (g + 1), :], in_=res[g][:]
+                )

@@ -32,12 +32,15 @@ def tile_mix_skip_fm_res_kernel(
 
         planes = keep.tile([P, 2, M], U8, name="planes", align_bytes=64)
         nc.vector.memset(planes[:].rearrange("p a n -> p (a n)").bitcast(I32), 0)
-        for a, scales in enumerate((wx_scales, wc_scales)):
+
+        def load_scales(queue, a, scales):
             for q in range(4):
-                nc.gpsimd.dma_start(
+                queue.dma_start(
                     out=planes[32 * q : 32 * q + 4, a, :].bitcast(I32),
                     in_=scales[0, 4 * q : 4 * q + 4, :].bitcast(I32),
                 )
+
+        load_scales(nc.gpsimd, 1, wc_scales)
 
         wc_raw = keep.tile([P, M], I32, name="wc_raw", align_bytes=64)
         nc.sync.dma_start(
@@ -49,6 +52,7 @@ def tile_mix_skip_fm_res_kernel(
         )
         x_raw = keep.tile([P, PACK, T], F32, name="x_raw", align_bytes=64)
         nc.sync.dma_start(out=x_raw[:], in_=x.rearrange("(p j) t -> p j t", j=PACK))
+        load_scales(nc.scalar, 0, wx_scales)
         c_raw = keep.tile([P, PACK, T], F32, name="c_raw", align_bytes=64)
         nc.sync.dma_start(out=c_raw[:], in_=c.rearrange("(p j) t -> p j t", j=PACK))
 
@@ -67,9 +71,14 @@ def tile_mix_skip_fm_res_kernel(
             out=wx[:], in_=wx_raw[:].rearrange("p (m s b) -> p s m b", s=ROWS, b=2)
         )
         w_scales = keep.tile([P, 2, ROWS, P], U8, name="w_scales", align_bytes=64)
-        nc.vector.tensor_copy(
-            out=w_scales[:], in_=planes[:].rearrange("p a (m s) -> p a s m", s=ROWS)
-        )
+
+        def permute_scales(a):
+            nc.vector.tensor_copy(
+                out=w_scales[:, a, :, :],
+                in_=planes[:, a, :].rearrange("p (m s) -> p s m", s=ROWS),
+            )
+
+        permute_scales(0)
 
         grouped = {}
         codes = {}
@@ -98,11 +107,12 @@ def tile_mix_skip_fm_res_kernel(
             )
 
         interleave(nc.scalar.copy, x_raw, ("x", 0))
-        interleave(nc.scalar.copy, x_raw, ("x", 1))
-        interleave(nc.scalar.copy, c_raw, ("c", 1))
+        interleave(nc.vector.tensor_copy, x_raw, ("x", 1))
         quantize(("x", 0))
-        interleave(nc.vector.tensor_copy, c_raw, ("c", 0))
         quantize(("x", 1))
+        permute_scales(1)
+        interleave(nc.scalar.copy, c_raw, ("c", 1))
+        interleave(nc.vector.tensor_copy, c_raw, ("c", 0))
         quantize(("c", 0))
         quantize(("c", 1))
 

@@ -18,7 +18,11 @@ PACK = 4
 ROWS = M // P
 N_TILE = 512
 HALVES = T // N_TILE
-GROUP = 3
+GROUPS = (1, 2, 3, 3, 3)
+BANKS = 8
+AHEAD = 4
+V_COLS = 352
+FOUR = 4
 
 
 def tile_mix_skip_fm_res_kernel(
@@ -31,7 +35,8 @@ def tile_mix_skip_fm_res_kernel(
         psum = ctx.enter_context(tc.psum_pool(name="psum", bufs=8))
 
         planes = keep.tile([P, 2, M], U8, name="planes", align_bytes=64)
-        nc.vector.memset(planes[:].rearrange("p a n -> p (a n)").bitcast(I32), 0)
+        for a in range(2):
+            nc.vector.memset(planes[:, a, :].bitcast(I32), 0)
 
         def load_scales(queue, a, scales):
             for q in range(4):
@@ -40,6 +45,7 @@ def tile_mix_skip_fm_res_kernel(
                     in_=scales[0, 4 * q : 4 * q + 4, :].bitcast(I32),
                 )
 
+        load_scales(nc.scalar, 0, wx_scales)
         load_scales(nc.gpsimd, 1, wc_scales)
 
         wc_raw = keep.tile([P, M], I32, name="wc_raw", align_bytes=64)
@@ -52,33 +58,53 @@ def tile_mix_skip_fm_res_kernel(
         )
         x_raw = keep.tile([P, PACK, T], F32, name="x_raw", align_bytes=64)
         nc.sync.dma_start(out=x_raw[:], in_=x.rearrange("(p j) t -> p j t", j=PACK))
-        load_scales(nc.scalar, 0, wx_scales)
         c_raw = keep.tile([P, PACK, T], F32, name="c_raw", align_bytes=64)
         nc.sync.dma_start(out=c_raw[:], in_=c.rearrange("(p j) t -> p j t", j=PACK))
 
         r_rows = r.rearrange("(p s) t -> p s t", s=ROWS)
         out_rows = out.rearrange("(p s) t -> p s t", s=ROWS)
         res = []
-        for g in range(ROWS // GROUP):
-            tile = keep.tile([P, GROUP, T], F32, name="res%d" % g, align_bytes=64)
-            nc.sync.dma_start(out=tile[:], in_=r_rows[:, GROUP * g : GROUP * (g + 1), :])
+        place = []
+        s0 = 0
+        for g, rows in enumerate(GROUPS):
+            tile = keep.tile([P, rows, T], F32, name="res%d" % g, align_bytes=64)
+            nc.sync.dma_start(out=tile[:], in_=r_rows[:, s0 : s0 + rows, :])
             res.append(tile)
+            place.extend((g, i) for i in range(rows))
+            s0 += rows
 
         wc = keep.tile([P, ROWS, P], I32, name="wc", align_bytes=64)
-        nc.vector.tensor_copy(out=wc[:], in_=wc_raw[:].rearrange("p (m s) -> p s m", s=ROWS))
         wx = keep.tile([P, ROWS, P, 2], U8, name="wx", align_bytes=64)
-        nc.vector.tensor_copy(
-            out=wx[:], in_=wx_raw[:].rearrange("p (m s b) -> p s m b", s=ROWS, b=2)
-        )
         w_scales = keep.tile([P, 2, ROWS, P], U8, name="w_scales", align_bytes=64)
 
-        def permute_scales(a):
+        def permute_wc(g):
             nc.vector.tensor_copy(
-                out=w_scales[:, a, :, :],
-                in_=planes[:, a, :].rearrange("p (m s) -> p s m", s=ROWS),
+                out=wc[:, FOUR * g : FOUR * (g + 1), :].rearrange("p s m -> p m s"),
+                in_=wc_raw[:].rearrange("p (m s) -> p m s", s=ROWS)[
+                    :, :, FOUR * g : FOUR * (g + 1)
+                ],
             )
 
-        permute_scales(0)
+        def permute_wx(g):
+            nc.vector.tensor_copy(
+                out=wx[:, FOUR * g : FOUR * (g + 1), :, :].rearrange("p s m b -> p m s b"),
+                in_=wx_raw[:].rearrange("p (m s b) -> p m s b", s=ROWS, b=2)[
+                    :, :, FOUR * g : FOUR * (g + 1), :
+                ],
+            )
+
+        def permute_scales(g):
+            for a in range(2):
+                nc.vector.tensor_copy(
+                    out=w_scales[:, a, FOUR * g : FOUR * (g + 1), :].rearrange("p s m -> p m s"),
+                    in_=planes[:, a, :].rearrange("p (m s) -> p m s", s=ROWS)[
+                        :, :, FOUR * g : FOUR * (g + 1)
+                    ],
+                )
+
+        for g in range(ROWS // FOUR):
+            permute_wc(g)
+            permute_wx(g)
 
         grouped = {}
         codes = {}
@@ -92,11 +118,11 @@ def tile_mix_skip_fm_res_kernel(
                 codes[key] = keep.tile([P, N_TILE], U32, name="codes_%s%d" % key, align_bytes=64)
                 bytes_[key] = keep.tile([P, N_TILE], U8, name="bytes_%s%d" % key, align_bytes=64)
 
-        def interleave(copy, raw, key):
-            h = key[1]
+        def interleave(copy, raw, key, lo=0, hi=N_TILE):
+            t0 = key[1] * N_TILE
             copy(
-                out=grouped[key][:],
-                in_=raw[:, :, h * N_TILE : (h + 1) * N_TILE].rearrange("p j t -> p t j"),
+                out=grouped[key][:, lo:hi, :].rearrange("p (c i) j -> p c j i", i=FOUR),
+                in_=raw[:, :, t0 + lo : t0 + hi].rearrange("p j (c i) -> p c j i", i=FOUR),
             )
 
         def quantize(key):
@@ -108,39 +134,56 @@ def tile_mix_skip_fm_res_kernel(
 
         interleave(nc.scalar.copy, x_raw, ("x", 0))
         interleave(nc.vector.tensor_copy, x_raw, ("x", 1))
-        quantize(("x", 0))
         quantize(("x", 1))
-        permute_scales(1)
-        interleave(nc.scalar.copy, c_raw, ("c", 1))
-        interleave(nc.vector.tensor_copy, c_raw, ("c", 0))
+        quantize(("x", 0))
+        permute_scales(0)
+        for h in range(HALVES):
+            interleave(nc.scalar.copy, c_raw, ("c", h), V_COLS, N_TILE)
+        for h in range(HALVES):
+            interleave(nc.vector.tensor_copy, c_raw, ("c", h), 0, V_COLS)
         quantize(("c", 0))
         quantize(("c", 1))
 
-        for s in range(ROWS):
-            g, i = divmod(s, GROUP)
-            for h in range(HALVES):
-                acc = psum.tile([P, N_TILE], F32, name="acc")
-                nc.tensor.matmul_mx(
-                    out=acc[:],
-                    lhsT=wx[:, s, :, :].rearrange("p m b -> p (m b)").bitcast(FP4X4),
-                    lhsT_scale=w_scales[:, 0, s, :],
-                    rhs=codes["x", h][:].bitcast(FP8X4),
-                    rhs_scale=bytes_["x", h][:],
-                    start=True,
-                    stop=False,
-                )
-                nc.tensor.matmul_mx(
-                    out=acc[:],
-                    lhsT=wc[:, s, :].bitcast(FP8X4),
-                    lhsT_scale=w_scales[:, 1, s, :],
-                    rhs=codes["c", h][:].bitcast(FP8X4),
-                    rhs_scale=bytes_["c", h][:],
-                    start=False,
-                    stop=True,
-                )
-                part = res[g][:, i, h * N_TILE : (h + 1) * N_TILE]
-                nc.vector.tensor_tensor(out=part, in0=acc[:], in1=part, op=mybir.AluOpType.add)
-            if i == GROUP - 1:
-                nc.sync.dma_start(
-                    out=out_rows[:, GROUP * g : GROUP * (g + 1), :], in_=res[g][:]
-                )
+        acc = {}
+
+        def x_pass(i):
+            s, h = divmod(i, HALVES)
+            bank = psum.tile([P, N_TILE], F32, name="acc")
+            acc[i] = bank
+            nc.tensor.matmul_mx(
+                out=bank[:],
+                lhsT=wx[:, s, :, :].rearrange("p m b -> p (m b)").bitcast(FP4X4),
+                lhsT_scale=w_scales[:, 0, s, :],
+                rhs=codes["x", h][:].bitcast(FP8X4),
+                rhs_scale=bytes_["x", h][:],
+                start=True,
+                stop=False,
+            )
+
+        def c_pass(i):
+            s, h = divmod(i, HALVES)
+            nc.tensor.matmul_mx(
+                out=acc[i][:],
+                lhsT=wc[:, s, :].bitcast(FP8X4),
+                lhsT_scale=w_scales[:, 1, s, :],
+                rhs=codes["c", h][:].bitcast(FP8X4),
+                rhs_scale=bytes_["c", h][:],
+                start=False,
+                stop=True,
+            )
+
+        tiles = ROWS * HALVES
+        for i in range(BANKS):
+            x_pass(i)
+        for i in range(tiles):
+            c_pass(i)
+            if BANKS <= i + AHEAD < tiles:
+                x_pass(i + AHEAD)
+            s, h = divmod(i, HALVES)
+            g, row = place[s]
+            part = res[g][:, row, h * N_TILE : (h + 1) * N_TILE]
+            nc.vector.tensor_tensor(out=part, in0=acc[i][:], in1=part, op=mybir.AluOpType.add)
+            if i in (1, 9):
+                permute_scales((i + 7) // 8)
+            if h == HALVES - 1 and row == GROUPS[g] - 1:
+                nc.sync.dma_start(out=out_rows[:, s - row : s + 1, :], in_=res[g][:])

@@ -18,11 +18,13 @@ PACK = 4
 ROWS = M // P
 N_TILE = 512
 HALVES = T // N_TILE
-GROUPS = (1, 2, 3, 3, 3)
+GROUPS = (3, 4, 5)
+STORES = (3, 4, 3, 2)
 BANKS = 8
 AHEAD = 4
 V_COLS = 352
 FOUR = 4
+WC_FIRST = 4
 
 
 def tile_mix_skip_fm_res_kernel(
@@ -34,19 +36,20 @@ def tile_mix_skip_fm_res_kernel(
         keep = ctx.enter_context(tc.tile_pool(name="keep", bufs=1))
         psum = ctx.enter_context(tc.psum_pool(name="psum", bufs=8))
 
-        planes = keep.tile([P, 2, M], U8, name="planes", align_bytes=64)
-        for a in range(2):
-            nc.vector.memset(planes[:, a, :].bitcast(I32), 0)
+        wx_plane = keep.tile([P, M], U8, name="wx_plane", align_bytes=64)
+        wc_plane = keep.tile([P, M], U8, name="wc_plane", align_bytes=64)
+        for plane in (wx_plane, wc_plane):
+            nc.vector.memset(plane[:].bitcast(I32), 0)
 
-        def load_scales(queue, a, scales):
+        def load_scales(plane, scales, first):
             for q in range(4):
-                queue.dma_start(
-                    out=planes[32 * q : 32 * q + 4, a, :].bitcast(I32),
+                p0 = 32 * q + first
+                nc.scalar.dma_start(
+                    out=plane[p0 : p0 + 4, :].bitcast(I32),
                     in_=scales[0, 4 * q : 4 * q + 4, :].bitcast(I32),
                 )
 
-        load_scales(nc.scalar, 0, wx_scales)
-        load_scales(nc.gpsimd, 1, wc_scales)
+        load_scales(wx_plane, wx_scales, 0)
 
         wc_raw = keep.tile([P, M], I32, name="wc_raw", align_bytes=64)
         nc.sync.dma_start(
@@ -60,6 +63,8 @@ def tile_mix_skip_fm_res_kernel(
         nc.sync.dma_start(out=x_raw[:], in_=x.rearrange("(p j) t -> p j t", j=PACK))
         c_raw = keep.tile([P, PACK, T], F32, name="c_raw", align_bytes=64)
         nc.sync.dma_start(out=c_raw[:], in_=c.rearrange("(p j) t -> p j t", j=PACK))
+
+        load_scales(wc_plane, wc_scales, WC_FIRST)
 
         r_rows = r.rearrange("(p s) t -> p s t", s=ROWS)
         out_rows = out.rearrange("(p s) t -> p s t", s=ROWS)
@@ -75,7 +80,8 @@ def tile_mix_skip_fm_res_kernel(
 
         wc = keep.tile([P, ROWS, P], I32, name="wc", align_bytes=64)
         wx = keep.tile([P, ROWS, P, 2], U8, name="wx", align_bytes=64)
-        w_scales = keep.tile([P, 2, ROWS, P], U8, name="w_scales", align_bytes=64)
+        wx_scale = keep.tile([P, ROWS, P], U8, name="wx_scale", align_bytes=64)
+        wc_scale = keep.tile([P, ROWS, P], U8, name="wc_scale", align_bytes=64)
 
         def permute_wc(g):
             nc.vector.tensor_copy(
@@ -94,10 +100,10 @@ def tile_mix_skip_fm_res_kernel(
             )
 
         def permute_scales(g):
-            for a in range(2):
+            for scale, plane in ((wx_scale, wx_plane), (wc_scale, wc_plane)):
                 nc.vector.tensor_copy(
-                    out=w_scales[:, a, FOUR * g : FOUR * (g + 1), :].rearrange("p s m -> p m s"),
-                    in_=planes[:, a, :].rearrange("p (m s) -> p m s", s=ROWS)[
+                    out=scale[:, FOUR * g : FOUR * (g + 1), :].rearrange("p s m -> p m s"),
+                    in_=plane[:].rearrange("p (m s) -> p m s", s=ROWS)[
                         :, :, FOUR * g : FOUR * (g + 1)
                     ],
                 )
@@ -143,6 +149,8 @@ def tile_mix_skip_fm_res_kernel(
             interleave(nc.vector.tensor_copy, c_raw, ("c", h), 0, V_COLS)
         quantize(("c", 0))
         quantize(("c", 1))
+        for g in range(1, ROWS // FOUR):
+            permute_scales(g)
 
         acc = {}
 
@@ -153,7 +161,7 @@ def tile_mix_skip_fm_res_kernel(
             nc.tensor.matmul_mx(
                 out=bank[:],
                 lhsT=wx[:, s, :, :].rearrange("p m b -> p (m b)").bitcast(FP4X4),
-                lhsT_scale=w_scales[:, 0, s, :],
+                lhsT_scale=wx_scale[:, s, :],
                 rhs=codes["x", h][:].bitcast(FP8X4),
                 rhs_scale=bytes_["x", h][:],
                 start=True,
@@ -165,7 +173,7 @@ def tile_mix_skip_fm_res_kernel(
             nc.tensor.matmul_mx(
                 out=acc[i][:],
                 lhsT=wc[:, s, :].bitcast(FP8X4),
-                lhsT_scale=w_scales[:, 1, s, :],
+                lhsT_scale=wc_scale[WC_FIRST:P, s, :],
                 rhs=codes["c", h][:].bitcast(FP8X4),
                 rhs_scale=bytes_["c", h][:],
                 start=False,
@@ -173,6 +181,7 @@ def tile_mix_skip_fm_res_kernel(
             )
 
         tiles = ROWS * HALVES
+        ends = {sum(STORES[: k + 1]): rows for k, rows in enumerate(STORES)}
         for i in range(BANKS):
             x_pass(i)
         for i in range(tiles):
@@ -183,7 +192,9 @@ def tile_mix_skip_fm_res_kernel(
             g, row = place[s]
             part = res[g][:, row, h * N_TILE : (h + 1) * N_TILE]
             nc.vector.tensor_tensor(out=part, in0=acc[i][:], in1=part, op=mybir.AluOpType.add)
-            if i in (1, 9):
-                permute_scales((i + 7) // 8)
-            if h == HALVES - 1 and row == GROUPS[g] - 1:
-                nc.sync.dma_start(out=out_rows[:, s - row : s + 1, :], in_=res[g][:])
+            if h == HALVES - 1 and s + 1 in ends:
+                rows = ends[s + 1]
+                nc.sync.dma_start(
+                    out=out_rows[:, s + 1 - rows : s + 1, :],
+                    in_=res[g][:, row + 1 - rows : row + 1, :],
+                )

@@ -18,8 +18,8 @@ PACK = 4
 ROWS = M // P
 N_TILE = 512
 HALVES = T // N_TILE
-GROUPS = (3, 4, 5)
-STORES = (3, 4, 3, 2)
+GROUPS = (2, 4, 6)
+STORES = (2, 4, 3, 3)
 BANKS = 8
 AHEAD = 4
 V_COLS = 352
@@ -34,6 +34,7 @@ def tile_mix_skip_fm_res_kernel(
     with ExitStack() as ctx:
         ctx.enter_context(tc.manual_schedule())
         keep = ctx.enter_context(tc.tile_pool(name="keep", bufs=1))
+        spill = ctx.enter_context(tc.tile_pool(name="spill", bufs=3))
         psum = ctx.enter_context(tc.psum_pool(name="psum", bufs=8))
 
         wx_plane = keep.tile([P, M], U8, name="wx_plane", align_bytes=64)
@@ -44,12 +45,10 @@ def tile_mix_skip_fm_res_kernel(
         def load_scales(plane, scales, first):
             for q in range(4):
                 p0 = 32 * q + first
-                nc.scalar.dma_start(
+                nc.sync.dma_start(
                     out=plane[p0 : p0 + 4, :].bitcast(I32),
                     in_=scales[0, 4 * q : 4 * q + 4, :].bitcast(I32),
                 )
-
-        load_scales(wx_plane, wx_scales, 0)
 
         wc_raw = keep.tile([P, M], I32, name="wc_raw", align_bytes=64)
         nc.sync.dma_start(
@@ -61,6 +60,7 @@ def tile_mix_skip_fm_res_kernel(
         )
         x_raw = keep.tile([P, PACK, T], F32, name="x_raw", align_bytes=64)
         nc.sync.dma_start(out=x_raw[:], in_=x.rearrange("(p j) t -> p j t", j=PACK))
+        load_scales(wx_plane, wx_scales, 0)
         c_raw = keep.tile([P, PACK, T], F32, name="c_raw", align_bytes=64)
         nc.sync.dma_start(out=c_raw[:], in_=c.rearrange("(p j) t -> p j t", j=PACK))
 
@@ -191,7 +191,16 @@ def tile_mix_skip_fm_res_kernel(
             s, h = divmod(i, HALVES)
             g, row = place[s]
             part = res[g][:, row, h * N_TILE : (h + 1) * N_TILE]
-            nc.vector.tensor_tensor(out=part, in0=acc[i][:], in1=part, op=mybir.AluOpType.add)
+            if i % 4 == 1:
+                copy = spill.tile([P, N_TILE], F32, name="copy")
+                nc.scalar.copy(out=copy[:], in_=acc[i][:])
+                nc.gpsimd.tensor_tensor(
+                    out=part, in0=copy[:], in1=part, op=mybir.AluOpType.add
+                )
+            else:
+                nc.vector.tensor_tensor(
+                    out=part, in0=acc[i][:], in1=part, op=mybir.AluOpType.add
+                )
             if h == HALVES - 1 and s + 1 in ends:
                 rows = ends[s + 1]
                 nc.sync.dma_start(

from contextlib import ExitStack

import concourse.mybir as mybir

K, L, M, T = 512, 512, 1536, 1024
FLOPS = 2 * M * T * (K + L)

F32 = mybir.dt.float32
BF16 = mybir.dt.bfloat16
I32 = mybir.dt.int32
U32 = mybir.dt.uint32
U8 = mybir.dt.uint8
FP8X4 = mybir.dt.float8_e4m3fn_x4
FP4X4 = mybir.dt.float4_e2m1fn_x4

P = 128
PACK = 4
ROWS = M // P
N_TILE = 512
HALVES = T // N_TILE
GROUPS = (2, 4, 6)
STORES = (2, 4, 3, 3)
BANKS = 8
AHEAD = 4
V_COLS = 352
FOUR = 4
WC_FIRST = 4


def tile_mix_skip_fm_res_kernel(
    tc, x, c, wx_words, wx_scales, wc_words, wc_scales, r, out
):
    nc = tc.nc
    with ExitStack() as ctx:
        ctx.enter_context(tc.manual_schedule())
        keep = ctx.enter_context(tc.tile_pool(name="keep", bufs=1))
        spill = ctx.enter_context(tc.tile_pool(name="spill", bufs=3))
        psum = ctx.enter_context(tc.psum_pool(name="psum", bufs=8))

        wx_plane = keep.tile([P, M], U8, name="wx_plane", align_bytes=64)
        wc_plane = keep.tile([P, M], U8, name="wc_plane", align_bytes=64)
        for plane in (wx_plane, wc_plane):
            nc.vector.memset(plane[:].bitcast(I32), 0)

        def load_scales(plane, scales, first):
            for q in range(4):
                p0 = 32 * q + first
                nc.sync.dma_start(
                    out=plane[p0 : p0 + 4, :].bitcast(I32),
                    in_=scales[0, 4 * q : 4 * q + 4, :].bitcast(I32),
                )

        wc_raw = keep.tile([P, M], I32, name="wc_raw", align_bytes=64)
        nc.sync.dma_start(
            out=wc_raw[:], in_=wc_words.rearrange("a p n i -> (a p) (n i)").bitcast(I32)
        )
        wx_raw = keep.tile([P, 2 * M], U8, name="wx_raw", align_bytes=64)
        nc.sync.dma_start(
            out=wx_raw[:].bitcast(I32), in_=wx_words.rearrange("a p b -> (a p) b").bitcast(I32)
        )
        x_raw = keep.tile([P, PACK, T], F32, name="x_raw", align_bytes=64)
        nc.sync.dma_start(out=x_raw[:], in_=x.rearrange("(p j) t -> p j t", j=PACK))
        load_scales(wx_plane, wx_scales, 0)
        c_raw = keep.tile([P, PACK, T], F32, name="c_raw", align_bytes=64)
        nc.sync.dma_start(out=c_raw[:], in_=c.rearrange("(p j) t -> p j t", j=PACK))

        load_scales(wc_plane, wc_scales, WC_FIRST)

        r_rows = r.rearrange("(p s) t -> p s t", s=ROWS)
        out_rows = out.rearrange("(p s) t -> p s t", s=ROWS)
        res = []
        place = []
        s0 = 0
        for g, rows in enumerate(GROUPS):
            tile = keep.tile([P, rows, T], F32, name="res%d" % g, align_bytes=64)
            nc.sync.dma_start(out=tile[:], in_=r_rows[:, s0 : s0 + rows, :])
            res.append(tile)
            place.extend((g, i) for i in range(rows))
            s0 += rows

        wc = keep.tile([P, ROWS, P], I32, name="wc", align_bytes=64)
        wx = keep.tile([P, ROWS, P, 2], U8, name="wx", align_bytes=64)
        wx_scale = keep.tile([P, ROWS, P], U8, name="wx_scale", align_bytes=64)
        wc_scale = keep.tile([P, ROWS, P], U8, name="wc_scale", align_bytes=64)

        def permute_wc(g):
            nc.vector.tensor_copy(
                out=wc[:, FOUR * g : FOUR * (g + 1), :].rearrange("p s m -> p m s"),
                in_=wc_raw[:].rearrange("p (m s) -> p m s", s=ROWS)[
                    :, :, FOUR * g : FOUR * (g + 1)
                ],
            )

        def permute_wx(g):
            nc.vector.tensor_copy(
                out=wx[:, FOUR * g : FOUR * (g + 1), :, :].rearrange("p s m b -> p m s b"),
                in_=wx_raw[:].rearrange("p (m s b) -> p m s b", s=ROWS, b=2)[
                    :, :, FOUR * g : FOUR * (g + 1), :
                ],
            )

        def permute_scales(g):
            for scale, plane in ((wx_scale, wx_plane), (wc_scale, wc_plane)):
                nc.vector.tensor_copy(
                    out=scale[:, FOUR * g : FOUR * (g + 1), :].rearrange("p s m -> p m s"),
                    in_=plane[:].rearrange("p (m s) -> p m s", s=ROWS)[
                        :, :, FOUR * g : FOUR * (g + 1)
                    ],
                )

        for g in range(ROWS // FOUR):
            permute_wc(g)
            permute_wx(g)

        grouped = {}
        codes = {}
        bytes_ = {}
        for name in ("x", "c"):
            for h in range(HALVES):
                key = (name, h)
                grouped[key] = keep.tile(
                    [P, N_TILE, PACK], BF16, name="grouped_%s%d" % key, align_bytes=64
                )
                codes[key] = keep.tile([P, N_TILE], U32, name="codes_%s%d" % key, align_bytes=64)
                bytes_[key] = keep.tile([P, N_TILE], U8, name="bytes_%s%d" % key, align_bytes=64)

        def interleave(copy, raw, key, lo=0, hi=N_TILE):
            t0 = key[1] * N_TILE
            copy(
                out=grouped[key][:, lo:hi, :].rearrange("p (c i) j -> p c j i", i=FOUR),
                in_=raw[:, :, t0 + lo : t0 + hi].rearrange("p j (c i) -> p c j i", i=FOUR),
            )

        def quantize(key):
            nc.vector.quantize_mx(
                out=codes[key][:].bitcast(FP8X4),
                scales=bytes_[key][:],
                in_=grouped[key][:].rearrange("p t j -> p (t j)"),
            )

        interleave(nc.scalar.copy, x_raw, ("x", 0))
        interleave(nc.vector.tensor_copy, x_raw, ("x", 1))
        quantize(("x", 1))
        quantize(("x", 0))
        permute_scales(0)
        for h in range(HALVES):
            interleave(nc.scalar.copy, c_raw, ("c", h), V_COLS, N_TILE)
        for h in range(HALVES):
            interleave(nc.vector.tensor_copy, c_raw, ("c", h), 0, V_COLS)
        quantize(("c", 0))
        quantize(("c", 1))
        for g in range(1, ROWS // FOUR):
            permute_scales(g)

        acc = {}

        def x_pass(i):
            s, h = divmod(i, HALVES)
            bank = psum.tile([P, N_TILE], F32, name="acc")
            acc[i] = bank
            nc.tensor.matmul_mx(
                out=bank[:],
                lhsT=wx[:, s, :, :].rearrange("p m b -> p (m b)").bitcast(FP4X4),
                lhsT_scale=wx_scale[:, s, :],
                rhs=codes["x", h][:].bitcast(FP8X4),
                rhs_scale=bytes_["x", h][:],
                start=True,
                stop=False,
            )

        def c_pass(i):
            s, h = divmod(i, HALVES)
            nc.tensor.matmul_mx(
                out=acc[i][:],
                lhsT=wc[:, s, :].bitcast(FP8X4),
                lhsT_scale=wc_scale[WC_FIRST:P, s, :],
                rhs=codes["c", h][:].bitcast(FP8X4),
                rhs_scale=bytes_["c", h][:],
                start=False,
                stop=True,
            )

        tiles = ROWS * HALVES
        ends = {sum(STORES[: k + 1]): rows for k, rows in enumerate(STORES)}
        for i in range(BANKS):
            x_pass(i)
        for i in range(tiles):
            c_pass(i)
            if BANKS <= i + AHEAD < tiles:
                x_pass(i + AHEAD)
            s, h = divmod(i, HALVES)
            g, row = place[s]
            part = res[g][:, row, h * N_TILE : (h + 1) * N_TILE]
            if i % 4 == 1:
                copy = spill.tile([P, N_TILE], F32, name="copy")
                nc.scalar.copy(out=copy[:], in_=acc[i][:])
                nc.gpsimd.tensor_tensor(
                    out=part, in0=copy[:], in1=part, op=mybir.AluOpType.add
                )
            else:
                nc.vector.tensor_tensor(
                    out=part, in0=acc[i][:], in1=part, op=mybir.AluOpType.add
                )
            if h == HALVES - 1 and s + 1 in ends:
                rows = ends[s + 1]
                nc.sync.dma_start(
                    out=out_rows[:, s + 1 - rows : s + 1, :],
                    in_=res[g][:, row + 1 - rows : row + 1, :],
                )
